import numpy as np
import ml_dtypes

BF16 = ml_dtypes.bfloat16


def bf(x):
    return np.asarray(x, np.float32).astype(BF16)


def f32(x):
    return np.asarray(x, np.float32)


def f64(x):
    return np.asarray(x).astype(np.float64)


def striped(idx):
    return np.tile(idx.reshape(-1, 16).T, (8, 1))


S, K, M, N, D, V = 1024, 128, 512, 2048, 4, 512


def setup_inputs():
    return {"table": bf(np.random.standard_normal((S, K))), "w": bf(np.random.standard_normal((K, M)) / np.sqrt(D * K)), "c": f32(0.2 + 0.8 * np.random.random_sample((1, V))), "offs": striped(np.random.permutation(np.tile(np.arange(S), 2))[:N])}


def reference(table, w, c, offs):
    idx = offs[:16].T.reshape(-1)
    x = f64(table)[idx].T
    y = f64(w).T @ sum(x[:, t * V : (t + 1) * V] for t in range(D))
    return y * f64(c)

@@ -1,0 +1,58 @@
+import concourse.mybir as mybir
+from concourse.masks import make_identity
+
+S, K, M, V, T = 1024, 128, 512, 512, 4
+P = 128
+HALVES = 2
+HALF = S // HALVES
+ROWS = HALF // P
+BLOCKS = M // P
+PIECE_COLS = V // 16
+BF16, F32, U16 = mybir.dt.bfloat16, mybir.dt.float32, mybir.dt.uint16
+
+FLOPS = 2 * K * M * V + (T - 1) * K * V + M * V
+
+
+def tile_gather_matmul_kernel(tc, table, w, c, offs, out):
+    nc = tc.nc
+    with (
+        tc.tile_pool(name="held", bufs=1) as held,
+        tc.tile_pool(name="results", bufs=BLOCKS) as results,
+        tc.psum_pool(name="turned", bufs=HALVES) as turned_pool,
+        tc.psum_pool(name="sums", bufs=BLOCKS) as sums_pool,
+    ):
+        nodes = held.tile([P, HALVES, ROWS, K], BF16, name="nodes")
+        nc.sync.dma_start(nodes[:], table.rearrange("(h p r) k -> p h r k", h=HALVES, p=P, r=ROWS))
+        offsets = held.tile([P, T * PIECE_COLS], U16, name="offsets")
+        nc.sync.dma_start(offsets[:], offs)
+        weights = held.tile([K, M], BF16, name="weights")
+        nc.scalar.dma_start(weights[:], w)
+        factors = held.tile([P, V], F32, name="factors")
+        nc.scalar.dma_start(factors[:], c[0, :].partition_broadcast(P))
+
+        identity = held.tile([P, P], BF16, name="identity")
+        make_identity(nc, identity[:])
+
+        features_first = held.tile([K, S], BF16, name="features_first")
+        for h in range(HALVES):
+            turned = turned_pool.tile([K, ROWS, P], BF16, name="turned")
+            for r in range(ROWS):
+                nc.tensor.transpose(turned[:, r, :], nodes[:, h, r, :], identity[:])
+            nc.vector.tensor_copy(
+                features_first[:, h * HALF : (h + 1) * HALF].rearrange("k (p r) -> k p r", r=ROWS),
+                turned[:].rearrange("k r p -> k p r"),
+            )
+
+        for m in range(BLOCKS):
+            sums = sums_pool.tile([P, V], F32, name="sums")
+            for t in range(T):
+                nc.tensor.matmul(
+                    sums[:],
+                    weights[:, m * P : (m + 1) * P],
+                    features_first[:].indirect(offsets[:, t * PIECE_COLS : (t + 1) * PIECE_COLS]),
+                    start=t == 0,
+                    stop=t == T - 1,
+                )
+            result = results.tile([P, V], F32, name="result")
+            nc.vector.tensor_tensor(result[:], sums[:], factors[:], mybir.AluOpType.mult)
+            nc.sync.dma_start(out[m * P : (m + 1) * P, :], result[:])

@@ -26,9 +26,9 @@ def tile_gather_matmul_kernel(tc, table, w, c, offs, out):
         offsets = held.tile([P, T * PIECE_COLS], U16, name="offsets")
         nc.sync.dma_start(offsets[:], offs)
         weights = held.tile([K, M], BF16, name="weights")
-        nc.scalar.dma_start(weights[:], w)
+        nc.sync.dma_start(weights[:], w)
         factors = held.tile([P, V], F32, name="factors")
-        nc.scalar.dma_start(factors[:], c[0, :].partition_broadcast(P))
+        nc.sync.dma_start(factors[:], c[0, :].partition_broadcast(P))
 
         identity = held.tile([P, P], BF16, name="identity")
         make_identity(nc, identity[:])
@@ -38,10 +38,10 @@ def tile_gather_matmul_kernel(tc, table, w, c, offs, out):
             turned = turned_pool.tile([K, ROWS, P], BF16, name="turned")
             for r in range(ROWS):
                 nc.tensor.transpose(turned[:, r, :], nodes[:, h, r, :], identity[:])
-            nc.vector.tensor_copy(
-                features_first[:, h * HALF : (h + 1) * HALF].rearrange("k (p r) -> k p r", r=ROWS),
-                turned[:].rearrange("k r p -> k p r"),
-            )
+            source = turned[:].rearrange("k r p -> k p r")
+            target = features_first[:, h * HALF : (h + 1) * HALF].rearrange("k (p r) -> k p r", r=ROWS)
+            nc.vector.tensor_copy(target[:, : P // 2, :], source[:, : P // 2, :])
+            nc.scalar.copy(target[:, P // 2 :, :], source[:, P // 2 :, :])
 
         for m in range(BLOCKS):
             sums = sums_pool.tile([P, V], F32, name="sums")
@@ -54,5 +54,6 @@ def tile_gather_matmul_kernel(tc, table, w, c, offs, out):
                     stop=t == T - 1,
                 )
             result = results.tile([P, V], F32, name="result")
-            nc.vector.tensor_tensor(result[:], sums[:], factors[:], mybir.AluOpType.mult)
-            nc.sync.dma_start(out[m * P : (m + 1) * P, :], result[:])
+            for queue, part in ((nc.sync, slice(0, V // 2)), (nc.scalar, slice(V // 2, V))):
+                nc.vector.tensor_tensor(result[:, part], sums[:, part], factors[:, part], mybir.AluOpType.mult)
+                queue.dma_start(out[m * P : (m + 1) * P, part], result[:, part])

@@ -22,7 +22,7 @@ def tile_gather_matmul_kernel(tc, table, w, c, offs, out):
         tc.psum_pool(name="sums", bufs=BLOCKS) as sums_pool,
     ):
         nodes = held.tile([P, HALVES, ROWS, K], BF16, name="nodes")
-        nc.sync.dma_start(nodes[:], table.rearrange("(h p r) k -> p h r k", h=HALVES, p=P, r=ROWS))
+        nc.sync.dma_start(nodes[:], table.rearrange("(h r p) k -> p h r k", h=HALVES, p=P, r=ROWS))
         offsets = held.tile([P, T * PIECE_COLS], U16, name="offsets")
         nc.sync.dma_start(offsets[:], offs)
         weights = held.tile([K, M], BF16, name="weights")
@@ -35,13 +35,10 @@ def tile_gather_matmul_kernel(tc, table, w, c, offs, out):
 
         features_first = held.tile([K, S], BF16, name="features_first")
         for h in range(HALVES):
-            turned = turned_pool.tile([K, ROWS, P], BF16, name="turned")
+            turned = turned_pool.tile([K, HALF], BF16, name="turned")
             for r in range(ROWS):
-                nc.tensor.transpose(turned[:, r, :], nodes[:, h, r, :], identity[:])
-            source = turned[:].rearrange("k r p -> k p r")
-            target = features_first[:, h * HALF : (h + 1) * HALF].rearrange("k (p r) -> k p r", r=ROWS)
-            nc.vector.tensor_copy(target[:, : P // 2, :], source[:, : P // 2, :])
-            nc.scalar.copy(target[:, P // 2 :, :], source[:, P // 2 :, :])
+                nc.tensor.transpose(turned[:, r * P : (r + 1) * P], nodes[:, h, r, :], identity[:])
+            nc.vector.tensor_copy(features_first[:, h * HALF : (h + 1) * HALF], turned[:])
 
         for m in range(BLOCKS):
             sums = sums_pool.tile([P, V], F32, name="sums")

import concourse.mybir as mybir
from concourse.masks import make_identity

S, K, M, V, T = 1024, 128, 512, 512, 4
P = 128
HALVES = 2
HALF = S // HALVES
ROWS = HALF // P
BLOCKS = M // P
PIECE_COLS = V // 16
BF16, F32, U16 = mybir.dt.bfloat16, mybir.dt.float32, mybir.dt.uint16

FLOPS = 2 * K * M * V + (T - 1) * K * V + M * V


def tile_gather_matmul_kernel(tc, table, w, c, offs, out):
    nc = tc.nc
    with (
        tc.tile_pool(name="held", bufs=1) as held,
        tc.tile_pool(name="results", bufs=BLOCKS) as results,
        tc.psum_pool(name="turned", bufs=HALVES) as turned_pool,
        tc.psum_pool(name="sums", bufs=BLOCKS) as sums_pool,
    ):
        nodes = held.tile([P, HALVES, ROWS, K], BF16, name="nodes")
        nc.sync.dma_start(nodes[:], table.rearrange("(h r p) k -> p h r k", h=HALVES, p=P, r=ROWS))
        offsets = held.tile([P, T * PIECE_COLS], U16, name="offsets")
        nc.sync.dma_start(offsets[:], offs)
        weights = held.tile([K, M], BF16, name="weights")
        nc.sync.dma_start(weights[:], w)
        factors = held.tile([P, V], F32, name="factors")
        nc.sync.dma_start(factors[:], c[0, :].partition_broadcast(P))

        identity = held.tile([P, P], BF16, name="identity")
        make_identity(nc, identity[:])

        features_first = held.tile([K, S], BF16, name="features_first")
        for h in range(HALVES):
            turned = turned_pool.tile([K, HALF], BF16, name="turned")
            for r in range(ROWS):
                nc.tensor.transpose(turned[:, r * P : (r + 1) * P], nodes[:, h, r, :], identity[:])
            nc.vector.tensor_copy(features_first[:, h * HALF : (h + 1) * HALF], turned[:])

        for m in range(BLOCKS):
            sums = sums_pool.tile([P, V], F32, name="sums")
            for t in range(T):
                nc.tensor.matmul(
                    sums[:],
                    weights[:, m * P : (m + 1) * P],
                    features_first[:].indirect(offsets[:, t * PIECE_COLS : (t + 1) * PIECE_COLS]),
                    start=t == 0,
                    stop=t == T - 1,
                )
            result = results.tile([P, V], F32, name="result")
            for queue, part in ((nc.sync, slice(0, V // 2)), (nc.scalar, slice(V // 2, V))):
                nc.vector.tensor_tensor(result[:, part], sums[:, part], factors[:, part], mybir.AluOpType.mult)
                queue.dma_start(out[m * P : (m + 1) * P, part], result[:, part])
